import numpy as np
import ml_dtypes


def mxq(x, axis, fmt="e4m3"):
    dtype, down = {"e4m3": (ml_dtypes.float8_e4m3fn, 7), "e5m2": (ml_dtypes.float8_e5m2, 14)}[fmt]
    v = np.moveaxis(np.asarray(x, np.float32).astype(ml_dtypes.bfloat16).astype(np.float64), axis, -1)
    blocks = v.reshape(v.shape[:-1] + (-1, 32))
    amax = np.abs(blocks).max(-1, keepdims=True)
    byte = np.maximum(np.where(amax > 0, np.frexp(amax)[1] - 1 + 127, 0) - down, 1)
    scale = np.exp2(byte - 127.0)
    codes = (blocks / scale).astype(np.float32).astype(dtype).astype(np.float64)
    return np.moveaxis((codes * scale).reshape(v.shape), -1, axis)


WIDE = False


def mx_kscale(k):
    if not WIDE:
        return np.ones(k)
    levels = np.array([10, -10, 5, -5, 0])
    if k % 512:
        return np.exp2(np.random.permutation(np.resize(levels, k // 32))).repeat(32)
    a = np.empty((k // 512, 16))
    for p in range(k // 512):
        a[p, :8] = np.random.permutation(np.resize(levels, 8))
        for g in range(8):
            far = levels[np.abs(levels - a[p, g]) >= 10]
            a[p, g + 8] = far[np.random.randint(len(far))]
    return np.exp2(a.ravel()).repeat(32)


def f64(x):
    return np.asarray(x).astype(np.float64)


def striped(idx):
    return np.tile(idx.reshape(-1, 16).T, (8, 1)).astype(np.uint16)


def unstriped(offs):
    return offs[:16].T.reshape(-1).astype(np.int64)


def striped8(idx):
    return np.concatenate([x.reshape(-1, 16).T for x in idx]).astype(np.uint16)


def runs(offs, k):
    lists = np.stack([offs[16 * r : 16 * r + 16].T.reshape(-1) for r in range(8)]).astype(np.int64)
    return lists[np.arange(k) % 512 // 64]


def pack_weight(w):
    k, n = w.shape
    w = f64(np.asarray(w, np.float32).astype(ml_dtypes.bfloat16)).reshape(k // 32, 32, n)
    amax = np.abs(w).max(1)
    byte = np.clip(np.where(amax > 0, np.frexp(amax)[1] - 1 + 127 - 7, 1), 1, 254)
    scaled = (w * np.exp2(127.0 - byte)[:, None, :]).reshape(k, n).astype(np.float32)
    words = np.ascontiguousarray(scaled.reshape(k // 512, 128, 4, n).transpose(0, 1, 3, 2)).astype(ml_dtypes.float8_e4m3fn).view(np.uint8)
    return words, np.ascontiguousarray(byte.astype(np.uint8).reshape(k // 512, 16, n))


def unpack_weight(words, scales):
    g, p, n, _ = words.shape
    vals = np.ascontiguousarray(words).view(ml_dtypes.float8_e4m3fn).astype(np.float64) * np.repeat(np.exp2(scales.astype(np.float64) - 127.0), 8, axis=1)[..., None]
    return vals.transpose(0, 1, 3, 2).reshape(g * 512, n)


def sigmoid(v):
    return 1.0 / (1.0 + np.exp(-np.maximum(v, -700.0)))


K, T, S, G, H, W = 512, 2048, 512, 2048, 512, 256


def setup_inputs():
    n = np.random.standard_normal
    s = mx_kscale(K)[:, None]
    packed_xT = pack_weight(n((K, T)) * s)
    packed_dT = pack_weight(n((K, G)) / s)
    perm = np.stack([np.random.permutation(S) for _ in range(8)])
    return {
        "x_words": packed_xT[0],
        "x_scales": packed_xT[1],
        "d_words": packed_dT[0],
        "d_scales": packed_dT[1],
        "gs": (np.random.uniform(0.5, 1.5, (K, 1)) * s).astype(np.float32),
        "offs": striped(np.random.permutation(T)[:S]),
        "k1": striped8(np.random.randint(0, G, (8, H))),
        "n1": striped8(perm[:, :W]),
        "n2": striped8(perm[:, W:]),
        "n3": striped8(np.stack([np.random.permutation(S) for _ in range(8)])),
        "n4": striped8(np.stack([np.random.permutation(S) for _ in range(8)])),
        "n5": striped8(np.stack([np.random.permutation(S) for _ in range(8)])),
    }


def reference(x_words, x_scales, d_words, d_scales, gs, offs, k1, n1, n2, n3, n4, n5):
    d_k1 = unpack_weight(d_words, d_scales)[np.arange(K)[:, None], runs(k1, K)]
    xq = unpack_weight(x_words, x_scales)[:, unstriped(offs)]
    h = 0.0625 * (d_k1.T @ xq)
    pa = h[np.arange(H)[:, None], runs(n1, H)]
    pb = h[np.arange(H)[:, None], runs(n2, H)]
    ra = pa - (0.5 * pb)
    ds = h.copy()
    ds[np.arange(H)[:, None], runs(n2, H)] = ra
    z = f64(gs) * (ds - (0.5 * (ds[np.arange(H)[:, None], runs(n3, H)])))
    h2 = 0.0625 * ((d_k1.T @ mxq(z, 0, "e4m3")))
    st = h2 * (sigmoid(h2[np.arange(H)[:, None], runs(n4, H)]))
    return st - (st[np.arange(H)[:, None], runs(n5, H)])

@@ -1,0 +1,185 @@
+from contextlib import ExitStack
+
+import concourse.mybir as mybir
+
+K, T, S, G, H, W = 512, 2048, 512, 2048, 512, 256
+FLOPS = 2 * 2 * K * H * S
+
+F32 = mybir.dt.float32
+BF16 = mybir.dt.bfloat16
+I32 = mybir.dt.int32
+U32 = mybir.dt.uint32
+U16 = mybir.dt.uint16
+U8 = mybir.dt.uint8
+FP8X4 = mybir.dt.float8_e4m3fn_x4
+ALU = mybir.AluOpType
+ACT = mybir.ActivationFunctionType
+
+P = 128
+PACK = 4
+HALF = 256
+Z_CHUNKS = (256, 128, 128)
+
+
+def tile_picked_ringfolddhopg_none_p_kernel(tc, x_words, x_scales, d_words, d_scales, gs, offs, k1, n1, n2, n3, n4, n5, out):
+    nc = tc.nc
+    with ExitStack() as ctx:
+        keep = ctx.enter_context(tc.tile_pool(name="keep", bufs=1))
+        psum = ctx.enter_context(tc.psum_pool(name="psum", bufs=1))
+
+        def sbuf(name, shape, dtype):
+            return keep.tile(shape, dtype, name=name, align_bytes=64)
+
+        def load_list(name, src):
+            tile = keep.tile(list(src.shape), U16, name=name)
+            nc.sync.dma_start(tile[:], src)
+            return tile
+
+        def load_scale_rows(name, src, clear):
+            tile = sbuf(name, [P, src.shape[2]], U8)
+            clear.memset(tile[:].bitcast(I32), 0)
+            nc.sync.dma_start(tile[0:P:8, :].bitcast(I32), src[0].bitcast(I32))
+            return tile
+
+        def load_words(name, src):
+            tile = sbuf(name, [P, src.shape[2]], I32)
+            nc.sync.dma_start(tile[:], src[0].rearrange("p c r -> p (c r)").bitcast(I32))
+            return tile
+
+        k1_list = load_list("k1_list", k1)
+        d_scale_table = load_scale_rows("d_scale_table", d_scales, nc.gpsimd)
+        offs_list = load_list("offs_list", offs)
+        x_scale_table = load_scale_rows("x_scale_table", x_scales, nc.vector)
+        gs_rows = sbuf("gs_rows", [P, PACK], F32)
+        nc.sync.dma_start(gs_rows[:], gs.rearrange("(p t) o -> p (t o)", t=PACK))
+        n1_list = load_list("n1_list", n1)
+        n2_list = load_list("n2_list", n2)
+        d_word_table = load_words("d_word_table", d_words)
+        x_word_table = load_words("x_word_table", x_words)
+        n3_list = load_list("n3_list", n3)
+        n4_list = load_list("n4_list", n4)
+        n5_list = load_list("n5_list", n5)
+
+        warm_in = sbuf("warm_in", [P, 1], F32)
+        warm_out = sbuf("warm_out", [P, 1], F32)
+        nc.gpsimd.memset(warm_in[:], 0.0)
+        nc.scalar.activation(warm_out[:], warm_in[:], ACT.Sigmoid)
+
+        planes = sbuf("planes", [P, H + S], U8)
+        nc.vector.memset(planes[:].bitcast(I32), 0)
+
+        d_scale_picked = sbuf("d_scale_picked", [P, H], U8)
+        x_scale_picked = sbuf("x_scale_picked", [P, S], U8)
+        scale_rows = sbuf("scale_rows", [P, H + S], U8)
+        nc.vector.tensor_copy(d_scale_picked[:], d_scale_table[:].indirect(k1_list[:]))
+        nc.vector.tensor_copy(x_scale_picked[:], x_scale_table[:].indirect(offs_list[:]))
+        nc.vector.tensor_copy(
+            scale_rows[:, 0:H].rearrange("p (t m) -> p t m", t=PACK),
+            d_scale_picked[:].rearrange("p (m t) -> p t m", t=PACK),
+        )
+        nc.vector.tensor_copy(scale_rows[:, H : H + S].bitcast(I32), x_scale_picked[:].bitcast(I32))
+        for r in range(4):
+            nc.scalar.dma_start(planes[r:P:32, :].bitcast(I32), scale_rows[8 * r : P : 32, :].bitcast(I32))
+
+        d_picked = sbuf("d_picked", [P, H], U32)
+        d_codes = sbuf("d_codes", [P, H], U32)
+        x_codes = sbuf("x_codes", [P, S], U32)
+        nc.vector.tensor_copy(d_picked[:], d_word_table[:].bitcast(U32).indirect(k1_list[:]))
+        nc.vector.tensor_copy(
+            d_codes[:].rearrange("p (t m) -> p t m", t=PACK),
+            d_picked[:].rearrange("p (m t) -> p t m", t=PACK),
+        )
+        nc.vector.tensor_copy(x_codes[:], x_word_table[:].bitcast(U32).indirect(offs_list[:]))
+
+        row_factor = sbuf("row_factor", [P, PACK], F32)
+        nc.gpsimd.tensor_scalar(row_factor[:], gs_rows[:], -0.03125, 0.0, ALU.mult, ALU.add)
+
+        def product(acc, t, codes, scales):
+            cols = slice(t * P, (t + 1) * P)
+            nc.tensor.matmul_mx(
+                out=acc,
+                lhsT=d_codes[:, cols].bitcast(FP8X4),
+                lhsT_scale=planes[:, cols],
+                rhs=codes.bitcast(FP8X4),
+                rhs_scale=scales,
+                start=True,
+                stop=True,
+            )
+
+        def bank():
+            return psum.tile([P, S], F32, name="bank", bufs=8)
+
+        halves = [slice(0, HALF), slice(HALF, S)]
+        list_halves = [slice(0, HALF // 16), slice(HALF // 16, S // 16)]
+        whole, list_whole = [slice(0, S)], [slice(0, S // 16)]
+
+        ds = [sbuf("ds%d" % t, [P, S], F32) for t in range(PACK)]
+        h2_window = [sbuf("h2_window%d" % t, [P, 2 * S], F32) for t in range(PACK)]
+        st_window = [sbuf("st_window%d" % t, [P, 2 * S], F32) for t in range(PACK)]
+        for t in range(PACK):
+            factor = row_factor[:, t : t + 1]
+            if t == 0:
+                accs = [bank(), bank()]
+                for acc, cols in zip(accs, halves):
+                    product(acc[:, 0:HALF], t, x_codes[:, cols], planes[:, H + cols.start : H + cols.stop])
+                nc.scalar.activation(ds[t][:, halves[0]], accs[0][:, 0:HALF], ACT.Copy, scale=factor)
+                nc.vector.tensor_scalar(ds[t][:, halves[1]], accs[1][:, 0:HALF], factor, None, ALU.mult)
+            else:
+                acc = bank()
+                product(acc[:], t, x_codes[:], planes[:, H : H + S])
+                nc.scalar.activation(ds[t][:], acc[:], ACT.Copy, scale=factor)
+        for t in range(PACK):
+            pa = st_window[t][:, S : S + W]
+            pb = st_window[t][:, S + W : 2 * S]
+            nc.vector.tensor_copy(pa, ds[t][:].indirect(n1_list[:]))
+            nc.vector.tensor_scalar(pb, ds[t][:].indirect(n2_list[:]), -0.5, 0.0, ALU.mult, ALU.add)
+            nc.vector.tensor_tensor(ds[t][:].indirect(n2_list[:]), pa, pb, ALU.add)
+            nc.scalar.activation(h2_window[t][:, S : 2 * S], ds[t][:], ACT.Copy, scale=2.0)
+
+        c0 = 0
+        for c, n in enumerate(Z_CHUNKS):
+            last = c == len(Z_CHUNKS) - 1
+            cols = slice(c0, c0 + n)
+            z = sbuf("z%d" % c, [P, PACK, n], F32)
+            for t in range(PACK):
+                nc.vector.tensor_tensor(
+                    z[:, t, :],
+                    ds[t][:].indirect(n3_list[:, c0 // 16 : (c0 + n) // 16]),
+                    h2_window[t][:, S + c0 : S + c0 + n],
+                    ALU.subtract,
+                )
+            z_bf = sbuf("z_bf%d" % c, [P, n * PACK], BF16)
+            dst = z_bf[:].rearrange("p (c i t) -> p c t i", i=4, t=PACK)
+            src = z[:].rearrange("p t (c i) -> p c t i", i=4)
+            if last:
+                nc.vector.tensor_copy(dst, src)
+            else:
+                nc.scalar.copy(dst, src)
+            z_codes = sbuf("z_codes%d" % c, [P, n], U32)
+            z_scales = sbuf("z_scales%d" % c, [P, n], U8)
+            nc.vector.quantize_mx(out=z_codes[:].bitcast(FP8X4), scales=z_scales[:], in_=z_bf[:])
+            for t in range(PACK):
+                acc = bank()
+                product(acc[:, 0:n], t, z_codes[:], z_scales[:])
+                if last and t > 0:
+                    nc.vector.tensor_scalar(h2_window[t][:, cols], acc[:, 0:n], 0.0625, None, ALU.mult)
+                else:
+                    nc.scalar.activation(h2_window[t][:, cols], acc[:, 0:n], ACT.Copy, scale=0.0625)
+            c0 += n
+
+        out_rows = out.rearrange("(p t) j -> p t j", t=PACK)
+        for t in range(PACK):
+            gate = sbuf("gate%d" % t, [P, S], F32)
+            minus_st_copy = sbuf("minus_st_copy%d" % t, [P, S], F32)
+            result = sbuf("result%d" % t, [P, S], F32)
+            for cols, entries in zip(halves, list_halves) if t == 0 else zip(whole, list_whole):
+                nc.scalar.activation(gate[:, cols], h2_window[t][:].indirect(n4_list[:, entries]), ACT.Sigmoid)
+                nc.vector.scalar_tensor_tensor(
+                    st_window[t][:, cols], h2_window[t][:, cols], -1.0, gate[:, cols], ALU.mult, ALU.mult
+                )
+                nc.scalar.copy(minus_st_copy[:, cols], st_window[t][:, cols])
+            for cols, entries in zip(halves, list_halves) if t == PACK - 1 else zip(whole, list_whole):
+                nc.vector.tensor_tensor(
+                    result[:, cols], st_window[t][:].indirect(n5_list[:, entries]), minus_st_copy[:, cols], ALU.subtract
+                )
+                nc.sync.dma_start(out_rows[:, t, cols], result[:, cols])

@@ -35,10 +35,11 @@ def tile_picked_ringfolddhopg_none_p_kernel(tc, x_words, x_scales, d_words, d_sc
             nc.sync.dma_start(tile[:], src)
             return tile
 
-        def load_scale_rows(name, src, clear):
+        def load_scale_rows(name, src, clear, queue):
             tile = sbuf(name, [P, src.shape[2]], U8)
-            clear.memset(tile[:].bitcast(I32), 0)
-            nc.sync.dma_start(tile[0:P:8, :].bitcast(I32), src[0].bitcast(I32))
+            for engine, cols in clear:
+                engine.memset(tile[:, cols].bitcast(I32), 0)
+            queue.dma_start(tile[0:P:8, :].bitcast(I32), src[0].bitcast(I32))
             return tile
 
         def load_words(name, src):
@@ -46,40 +47,39 @@ def tile_picked_ringfolddhopg_none_p_kernel(tc, x_words, x_scales, d_words, d_sc
             nc.sync.dma_start(tile[:], src[0].rearrange("p c r -> p (c r)").bitcast(I32))
             return tile
 
+        halves = [slice(0, HALF), slice(HALF, S)]
+        list_halves = [slice(0, HALF // 16), slice(HALF // 16, S // 16)]
+        whole, list_whole = [slice(0, S)], [slice(0, S // 16)]
+
         k1_list = load_list("k1_list", k1)
-        d_scale_table = load_scale_rows("d_scale_table", d_scales, nc.gpsimd)
-        offs_list = load_list("offs_list", offs)
-        x_scale_table = load_scale_rows("x_scale_table", x_scales, nc.vector)
         gs_rows = sbuf("gs_rows", [P, PACK], F32)
-        nc.sync.dma_start(gs_rows[:], gs.rearrange("(p t) o -> p (t o)", t=PACK))
+        nc.scalar.dma_start(gs_rows[:], gs.rearrange("(p t) o -> p (t o)", t=PACK))
+        d_scale_table = load_scale_rows("d_scale_table", d_scales, [(nc.gpsimd, slice(0, 1280)), (nc.vector, slice(1280, G))], nc.scalar)
+        x_scale_table = load_scale_rows("x_scale_table", x_scales, [(nc.vector, slice(0, T))], nc.sync)
+        offs_list = load_list("offs_list", offs)
         n1_list = load_list("n1_list", n1)
-        n2_list = load_list("n2_list", n2)
         d_word_table = load_words("d_word_table", d_words)
         x_word_table = load_words("x_word_table", x_words)
+        n2_list = load_list("n2_list", n2)
         n3_list = load_list("n3_list", n3)
         n4_list = load_list("n4_list", n4)
         n5_list = load_list("n5_list", n5)
 
-        warm_in = sbuf("warm_in", [P, 1], F32)
         warm_out = sbuf("warm_out", [P, 1], F32)
-        nc.gpsimd.memset(warm_in[:], 0.0)
-        nc.scalar.activation(warm_out[:], warm_in[:], ACT.Sigmoid)
-
-        planes = sbuf("planes", [P, H + S], U8)
-        nc.vector.memset(planes[:].bitcast(I32), 0)
+        nc.scalar.activation(warm_out[:], gs_rows[:, 0:1], ACT.Sigmoid)
 
         d_scale_picked = sbuf("d_scale_picked", [P, H], U8)
         x_scale_picked = sbuf("x_scale_picked", [P, S], U8)
-        scale_rows = sbuf("scale_rows", [P, H + S], U8)
+        planes = sbuf("planes", [P, H + S], U8)
         nc.vector.tensor_copy(d_scale_picked[:], d_scale_table[:].indirect(k1_list[:]))
         nc.vector.tensor_copy(x_scale_picked[:], x_scale_table[:].indirect(offs_list[:]))
         nc.vector.tensor_copy(
-            scale_rows[:, 0:H].rearrange("p (t m) -> p t m", t=PACK),
+            planes[:, 0:H].rearrange("p (t m) -> p t m", t=PACK),
             d_scale_picked[:].rearrange("p (m t) -> p t m", t=PACK),
         )
-        nc.vector.tensor_copy(scale_rows[:, H : H + S].bitcast(I32), x_scale_picked[:].bitcast(I32))
-        for r in range(4):
-            nc.scalar.dma_start(planes[r:P:32, :].bitcast(I32), scale_rows[8 * r : P : 32, :].bitcast(I32))
+        nc.vector.tensor_copy(planes[:, H : H + S].bitcast(I32), x_scale_picked[:].bitcast(I32))
+        for r in range(1, 4):
+            nc.scalar.dma_start(planes[r:P:32, :].bitcast(I32), planes[8 * r : P : 32, :].bitcast(I32))
 
         d_picked = sbuf("d_picked", [P, H], U32)
         d_codes = sbuf("d_codes", [P, H], U32)
@@ -89,10 +89,15 @@ def tile_picked_ringfolddhopg_none_p_kernel(tc, x_words, x_scales, d_words, d_sc
             d_codes[:].rearrange("p (t m) -> p t m", t=PACK),
             d_picked[:].rearrange("p (m t) -> p t m", t=PACK),
         )
-        nc.vector.tensor_copy(x_codes[:], x_word_table[:].bitcast(U32).indirect(offs_list[:]))
+        for cols, entries in zip(halves, list_halves):
+            nc.vector.tensor_copy(x_codes[:, cols], x_word_table[:].bitcast(U32).indirect(offs_list[:, entries]))
 
-        row_factor = sbuf("row_factor", [P, PACK], F32)
-        nc.gpsimd.tensor_scalar(row_factor[:], gs_rows[:], -0.03125, 0.0, ALU.mult, ALU.add)
+        rows = [sbuf("rows%d" % t, [P, S + 16 if t == 0 else 2 * S], F32) for t in range(PACK)]
+        row_factor = [rows[(t - 1) % PACK][:, S : S + 1] for t in range(PACK)]
+        for t in range(PACK):
+            nc.vector.memset(rows[t][:, S:], 0.0)
+        for t in range(PACK):
+            nc.scalar.activation(row_factor[t], gs_rows[:, t : t + 1], ACT.Copy, scale=0.0625)
 
         def product(acc, t, codes, scales):
             cols = slice(t * P, (t + 1) * P)
@@ -109,46 +114,60 @@ def tile_picked_ringfolddhopg_none_p_kernel(tc, x_words, x_scales, d_words, d_sc
         def bank():
             return psum.tile([P, S], F32, name="bank", bufs=8)
 
-        halves = [slice(0, HALF), slice(HALF, S)]
-        list_halves = [slice(0, HALF // 16), slice(HALF // 16, S // 16)]
-        whole, list_whole = [slice(0, S)], [slice(0, S // 16)]
 
-        ds = [sbuf("ds%d" % t, [P, S], F32) for t in range(PACK)]
-        h2_window = [sbuf("h2_window%d" % t, [P, 2 * S], F32) for t in range(PACK)]
+        ds_half = [sbuf("ds_half%d" % t, [P, S], F32) for t in range(PACK)]
         st_window = [sbuf("st_window%d" % t, [P, 2 * S], F32) for t in range(PACK)]
         for t in range(PACK):
-            factor = row_factor[:, t : t + 1]
             if t == 0:
                 accs = [bank(), bank()]
                 for acc, cols in zip(accs, halves):
                     product(acc[:, 0:HALF], t, x_codes[:, cols], planes[:, H + cols.start : H + cols.stop])
-                nc.scalar.activation(ds[t][:, halves[0]], accs[0][:, 0:HALF], ACT.Copy, scale=factor)
-                nc.vector.tensor_scalar(ds[t][:, halves[1]], accs[1][:, 0:HALF], factor, None, ALU.mult)
+                nc.scalar.activation(rows[t][:, halves[0]], accs[0][:, 0:HALF], ACT.Copy, scale=row_factor[t])
+                nc.vector.tensor_scalar(rows[t][:, halves[1]], accs[1][:, 0:HALF], row_factor[t], None, ALU.mult)
             else:
                 acc = bank()
                 product(acc[:], t, x_codes[:], planes[:, H : H + S])
-                nc.scalar.activation(ds[t][:], acc[:], ACT.Copy, scale=factor)
-        for t in range(PACK):
-            pa = st_window[t][:, S : S + W]
-            pb = st_window[t][:, S + W : 2 * S]
-            nc.vector.tensor_copy(pa, ds[t][:].indirect(n1_list[:]))
-            nc.vector.tensor_scalar(pb, ds[t][:].indirect(n2_list[:]), -0.5, 0.0, ALU.mult, ALU.add)
-            nc.vector.tensor_tensor(ds[t][:].indirect(n2_list[:]), pa, pb, ALU.add)
-            nc.scalar.activation(h2_window[t][:, S : 2 * S], ds[t][:], ACT.Copy, scale=2.0)
+                nc.scalar.activation(rows[t][:, 0:S], acc[:], ACT.Copy, scale=row_factor[t])
+
+        def fetch_pair(t):
+            nc.vector.tensor_copy(st_window[t][:, S : S + W], rows[t][:].indirect(n1_list[:]))
+            nc.vector.tensor_scalar(st_window[t][:, S + W : 2 * S], rows[t][:].indirect(n2_list[:]), -0.5, 0.0, ALU.mult, ALU.add)
+
+        def put_back(t):
+            nc.vector.tensor_tensor(
+                rows[t][:].indirect(n2_list[:]), st_window[t][:, S : S + W], st_window[t][:, S + W : 2 * S], ALU.add
+            )
+            nc.scalar.activation(ds_half[t][:], rows[t][:, 0:S], ACT.Copy, scale=-0.5)
+
+        for t in range(PACK + 1):
+            if t < PACK:
+                fetch_pair(t)
+            if t > 0:
+                put_back(t - 1)
+
+        gate = [sbuf("gate%d" % t, [P, S], F32) for t in range(PACK)]
+
+        def leave_bank(t, accs, cols, engine):
+            if engine == "scalar":
+                nc.scalar.activation(rows[t][:, cols], accs[t][:, 0:HALF], ACT.Copy, scale=-0.0625 if t == 0 else 0.0625)
+            else:
+                nc.vector.tensor_scalar(rows[t][:, cols], accs[t][:, 0:HALF], 0.0625, None, ALU.mult)
 
         c0 = 0
         for c, n in enumerate(Z_CHUNKS):
             last = c == len(Z_CHUNKS) - 1
-            cols = slice(c0, c0 + n)
-            z = sbuf("z%d" % c, [P, PACK, n], F32)
+            if last:
+                z = keep.tile([P, PACK, n], F32, name="z_last", tag="z_bf0", align_bytes=64)
+            else:
+                z = sbuf("z%d" % c, [P, PACK, n], F32)
             for t in range(PACK):
                 nc.vector.tensor_tensor(
                     z[:, t, :],
-                    ds[t][:].indirect(n3_list[:, c0 // 16 : (c0 + n) // 16]),
-                    h2_window[t][:, S + c0 : S + c0 + n],
-                    ALU.subtract,
+                    ds_half[t][:].indirect(n3_list[:, c0 // 16 : (c0 + n) // 16]),
+                    rows[t][:, c0 : c0 + n],
+                    ALU.add,
                 )
-            z_bf = sbuf("z_bf%d" % c, [P, n * PACK], BF16)
+            z_bf = keep.tile([P, n * PACK], BF16, name="z_bf%d" % c, tag="z_bf%d" % min(c, 1), align_bytes=64)
             dst = z_bf[:].rearrange("p (c i t) -> p c t i", i=4, t=PACK)
             src = z[:].rearrange("p t (c i) -> p c t i", i=4)
             if last:
@@ -158,28 +177,48 @@ def tile_picked_ringfolddhopg_none_p_kernel(tc, x_words, x_scales, d_words, d_sc
             z_codes = sbuf("z_codes%d" % c, [P, n], U32)
             z_scales = sbuf("z_scales%d" % c, [P, n], U8)
             nc.vector.quantize_mx(out=z_codes[:].bitcast(FP8X4), scales=z_scales[:], in_=z_bf[:])
+            if c0 % HALF == 0:
+                accs = [bank() for t in range(PACK)]
             for t in range(PACK):
-                acc = bank()
-                product(acc[:, 0:n], t, z_codes[:], z_scales[:])
-                if last and t > 0:
-                    nc.vector.tensor_scalar(h2_window[t][:, cols], acc[:, 0:n], 0.0625, None, ALU.mult)
-                else:
-                    nc.scalar.activation(h2_window[t][:, cols], acc[:, 0:n], ACT.Copy, scale=0.0625)
+                product(accs[t][:, c0 % HALF : c0 % HALF + n], t, z_codes[:], z_scales[:])
             c0 += n
+            if c0 == HALF:
+                nc.scalar.activation(gate[0][:, halves[0]], accs[0][:, 0:HALF], ACT.Sigmoid, scale=0.0625)
+                for t in range(PACK):
+                    leave_bank(t, accs, halves[0], "scalar")
 
         out_rows = out.rearrange("(p t) j -> p t j", t=PACK)
-        for t in range(PACK):
-            gate = sbuf("gate%d" % t, [P, S], F32)
-            minus_st_copy = sbuf("minus_st_copy%d" % t, [P, S], F32)
-            result = sbuf("result%d" % t, [P, S], F32)
-            for cols, entries in zip(halves, list_halves) if t == 0 else zip(whole, list_whole):
-                nc.scalar.activation(gate[:, cols], h2_window[t][:].indirect(n4_list[:, entries]), ACT.Sigmoid)
-                nc.vector.scalar_tensor_tensor(
-                    st_window[t][:, cols], h2_window[t][:, cols], -1.0, gate[:, cols], ALU.mult, ALU.mult
-                )
-                nc.scalar.copy(minus_st_copy[:, cols], st_window[t][:, cols])
+        minus_st_copy = [sbuf("minus_st_copy%d" % t, [P, S], F32) for t in range(PACK)]
+        result = [sbuf("result%d" % t, [P, S], F32) for t in range(PACK)]
+
+        def gate_of(t):
+            nc.scalar.activation(gate[t][:], rows[t][:].indirect(n4_list[:]), ACT.Sigmoid)
+
+        def gated(t):
+            nc.vector.scalar_tensor_tensor(st_window[t][:, 0:S], rows[t][:, 0:S], -1.0, gate[t][:], ALU.mult, ALU.mult)
+
+        def difference(t):
+            nc.scalar.copy(minus_st_copy[t][:], st_window[t][:, 0:S])
             for cols, entries in zip(halves, list_halves) if t == PACK - 1 else zip(whole, list_whole):
                 nc.vector.tensor_tensor(
-                    result[:, cols], st_window[t][:].indirect(n5_list[:, entries]), minus_st_copy[:, cols], ALU.subtract
+                    result[t][:, cols], st_window[t][:].indirect(n5_list[:, entries]), minus_st_copy[t][:, cols], ALU.subtract
                 )
-                nc.sync.dma_start(out_rows[:, t, cols], result[:, cols])
+                nc.sync.dma_start(out_rows[:, t, cols], result[t][:, cols])
+
+        nc.scalar.activation(gate[0][:, halves[1]], accs[0][:, 0:HALF], ACT.Sigmoid, scale=0.0625)
+        leave_bank(0, accs, halves[1], "scalar")
+        leave_bank(1, accs, halves[1], "vector")
+        gate_of(1)
+        for cols, entries in zip(halves, list_halves):
+            nc.vector.tensor_tensor(st_window[0][:, cols], gate[0][:].indirect(n4_list[:, entries]), rows[0][:, cols], ALU.mult)
+        leave_bank(2, accs, halves[1], "vector")
+        gated(1)
+        difference(0)
+        gate_of(2)
+        gated(2)
+        difference(1)
+        leave_bank(3, accs, halves[1], "scalar")
+        gate_of(3)
+        gated(3)
+        difference(2)
+        difference(3)

@@ -153,13 +153,14 @@ def tile_picked_ringfolddhopg_none_p_kernel(tc, x_words, x_scales, d_words, d_sc
             else:
                 nc.vector.tensor_scalar(rows[t][:, cols], accs[t][:, 0:HALF], 0.0625, None, ALU.mult)
 
+        shared = sbuf("shared", [P, Z_CHUNKS[-1] + Z_CHUNKS[0] * PACK // 2], F32)
         c0 = 0
         for c, n in enumerate(Z_CHUNKS):
             last = c == len(Z_CHUNKS) - 1
             if last:
-                z = keep.tile([P, PACK, n], F32, name="z_last", tag="z_bf0", align_bytes=64)
+                z = shared[:, 0 : PACK * n].rearrange("p (t j) -> p t j", t=PACK)
             else:
-                z = sbuf("z%d" % c, [P, PACK, n], F32)
+                z = sbuf("z%d" % c, [P, PACK, n], F32)[:]
             for t in range(PACK):
                 nc.vector.tensor_tensor(
                     z[:, t, :],
@@ -167,16 +168,19 @@ def tile_picked_ringfolddhopg_none_p_kernel(tc, x_words, x_scales, d_words, d_sc
                     rows[t][:, c0 : c0 + n],
                     ALU.add,
                 )
-            z_bf = keep.tile([P, n * PACK], BF16, name="z_bf%d" % c, tag="z_bf%d" % min(c, 1), align_bytes=64)
-            dst = z_bf[:].rearrange("p (c i t) -> p c t i", i=4, t=PACK)
-            src = z[:].rearrange("p t (c i) -> p c t i", i=4)
+            if c == 0:
+                z_bf = shared[:, Z_CHUNKS[-1] :].bitcast(BF16)
+            else:
+                z_bf = keep.tile([P, n * PACK], BF16, name="z_bf%d" % c, tag="z_bf", align_bytes=64)[:]
+            dst = z_bf.rearrange("p (c i t) -> p c t i", i=4, t=PACK)
+            src = z.rearrange("p t (c i) -> p c t i", i=4)
             if last:
                 nc.vector.tensor_copy(dst, src)
             else:
                 nc.scalar.copy(dst, src)
             z_codes = sbuf("z_codes%d" % c, [P, n], U32)
             z_scales = sbuf("z_scales%d" % c, [P, n], U8)
-            nc.vector.quantize_mx(out=z_codes[:].bitcast(FP8X4), scales=z_scales[:], in_=z_bf[:])
+            nc.vector.quantize_mx(out=z_codes[:].bitcast(FP8X4), scales=z_scales[:], in_=z_bf)
             if c0 % HALF == 0:
                 accs = [bank() for t in range(PACK)]
             for t in range(PACK):

from contextlib import ExitStack

import concourse.mybir as mybir

K, T, S, G, H, W = 512, 2048, 512, 2048, 512, 256
FLOPS = 2 * 2 * K * H * S

F32 = mybir.dt.float32
BF16 = mybir.dt.bfloat16
I32 = mybir.dt.int32
U32 = mybir.dt.uint32
U16 = mybir.dt.uint16
U8 = mybir.dt.uint8
FP8X4 = mybir.dt.float8_e4m3fn_x4
ALU = mybir.AluOpType
ACT = mybir.ActivationFunctionType

P = 128
PACK = 4
HALF = 256
Z_CHUNKS = (256, 128, 128)


def tile_picked_ringfolddhopg_none_p_kernel(tc, x_words, x_scales, d_words, d_scales, gs, offs, k1, n1, n2, n3, n4, n5, out):
    nc = tc.nc
    with ExitStack() as ctx:
        keep = ctx.enter_context(tc.tile_pool(name="keep", bufs=1))
        psum = ctx.enter_context(tc.psum_pool(name="psum", bufs=1))

        def sbuf(name, shape, dtype):
            return keep.tile(shape, dtype, name=name, align_bytes=64)

        def load_list(name, src):
            tile = keep.tile(list(src.shape), U16, name=name)
            nc.sync.dma_start(tile[:], src)
            return tile

        def load_scale_rows(name, src, clear, queue):
            tile = sbuf(name, [P, src.shape[2]], U8)
            for engine, cols in clear:
                engine.memset(tile[:, cols].bitcast(I32), 0)
            queue.dma_start(tile[0:P:8, :].bitcast(I32), src[0].bitcast(I32))
            return tile

        def load_words(name, src):
            tile = sbuf(name, [P, src.shape[2]], I32)
            nc.sync.dma_start(tile[:], src[0].rearrange("p c r -> p (c r)").bitcast(I32))
            return tile

        halves = [slice(0, HALF), slice(HALF, S)]
        list_halves = [slice(0, HALF // 16), slice(HALF // 16, S // 16)]
        whole, list_whole = [slice(0, S)], [slice(0, S // 16)]

        k1_list = load_list("k1_list", k1)
        gs_rows = sbuf("gs_rows", [P, PACK], F32)
        nc.scalar.dma_start(gs_rows[:], gs.rearrange("(p t) o -> p (t o)", t=PACK))
        d_scale_table = load_scale_rows("d_scale_table", d_scales, [(nc.gpsimd, slice(0, 1280)), (nc.vector, slice(1280, G))], nc.scalar)
        x_scale_table = load_scale_rows("x_scale_table", x_scales, [(nc.vector, slice(0, T))], nc.sync)
        offs_list = load_list("offs_list", offs)
        n1_list = load_list("n1_list", n1)
        d_word_table = load_words("d_word_table", d_words)
        x_word_table = load_words("x_word_table", x_words)
        n2_list = load_list("n2_list", n2)
        n3_list = load_list("n3_list", n3)
        n4_list = load_list("n4_list", n4)
        n5_list = load_list("n5_list", n5)

        warm_out = sbuf("warm_out", [P, 1], F32)
        nc.scalar.activation(warm_out[:], gs_rows[:, 0:1], ACT.Sigmoid)

        d_scale_picked = sbuf("d_scale_picked", [P, H], U8)
        x_scale_picked = sbuf("x_scale_picked", [P, S], U8)
        planes = sbuf("planes", [P, H + S], U8)
        nc.vector.tensor_copy(d_scale_picked[:], d_scale_table[:].indirect(k1_list[:]))
        nc.vector.tensor_copy(x_scale_picked[:], x_scale_table[:].indirect(offs_list[:]))
        nc.vector.tensor_copy(
            planes[:, 0:H].rearrange("p (t m) -> p t m", t=PACK),
            d_scale_picked[:].rearrange("p (m t) -> p t m", t=PACK),
        )
        nc.vector.tensor_copy(planes[:, H : H + S].bitcast(I32), x_scale_picked[:].bitcast(I32))
        for r in range(1, 4):
            nc.scalar.dma_start(planes[r:P:32, :].bitcast(I32), planes[8 * r : P : 32, :].bitcast(I32))

        d_picked = sbuf("d_picked", [P, H], U32)
        d_codes = sbuf("d_codes", [P, H], U32)
        x_codes = sbuf("x_codes", [P, S], U32)
        nc.vector.tensor_copy(d_picked[:], d_word_table[:].bitcast(U32).indirect(k1_list[:]))
        nc.vector.tensor_copy(
            d_codes[:].rearrange("p (t m) -> p t m", t=PACK),
            d_picked[:].rearrange("p (m t) -> p t m", t=PACK),
        )
        for cols, entries in zip(halves, list_halves):
            nc.vector.tensor_copy(x_codes[:, cols], x_word_table[:].bitcast(U32).indirect(offs_list[:, entries]))

        rows = [sbuf("rows%d" % t, [P, S + 16 if t == 0 else 2 * S], F32) for t in range(PACK)]
        row_factor = [rows[(t - 1) % PACK][:, S : S + 1] for t in range(PACK)]
        for t in range(PACK):
            nc.vector.memset(rows[t][:, S:], 0.0)
        for t in range(PACK):
            nc.scalar.activation(row_factor[t], gs_rows[:, t : t + 1], ACT.Copy, scale=0.0625)

        def product(acc, t, codes, scales):
            cols = slice(t * P, (t + 1) * P)
            nc.tensor.matmul_mx(
                out=acc,
                lhsT=d_codes[:, cols].bitcast(FP8X4),
                lhsT_scale=planes[:, cols],
                rhs=codes.bitcast(FP8X4),
                rhs_scale=scales,
                start=True,
                stop=True,
            )

        def bank():
            return psum.tile([P, S], F32, name="bank", bufs=8)


        ds_half = [sbuf("ds_half%d" % t, [P, S], F32) for t in range(PACK)]
        st_window = [sbuf("st_window%d" % t, [P, 2 * S], F32) for t in range(PACK)]
        for t in range(PACK):
            if t == 0:
                accs = [bank(), bank()]
                for acc, cols in zip(accs, halves):
                    product(acc[:, 0:HALF], t, x_codes[:, cols], planes[:, H + cols.start : H + cols.stop])
                nc.scalar.activation(rows[t][:, halves[0]], accs[0][:, 0:HALF], ACT.Copy, scale=row_factor[t])
                nc.vector.tensor_scalar(rows[t][:, halves[1]], accs[1][:, 0:HALF], row_factor[t], None, ALU.mult)
            else:
                acc = bank()
                product(acc[:], t, x_codes[:], planes[:, H : H + S])
                nc.scalar.activation(rows[t][:, 0:S], acc[:], ACT.Copy, scale=row_factor[t])

        def fetch_pair(t):
            nc.vector.tensor_copy(st_window[t][:, S : S + W], rows[t][:].indirect(n1_list[:]))
            nc.vector.tensor_scalar(st_window[t][:, S + W : 2 * S], rows[t][:].indirect(n2_list[:]), -0.5, 0.0, ALU.mult, ALU.add)

        def put_back(t):
            nc.vector.tensor_tensor(
                rows[t][:].indirect(n2_list[:]), st_window[t][:, S : S + W], st_window[t][:, S + W : 2 * S], ALU.add
            )
            nc.scalar.activation(ds_half[t][:], rows[t][:, 0:S], ACT.Copy, scale=-0.5)

        for t in range(PACK + 1):
            if t < PACK:
                fetch_pair(t)
            if t > 0:
                put_back(t - 1)

        gate = [sbuf("gate%d" % t, [P, S], F32) for t in range(PACK)]

        def leave_bank(t, accs, cols, engine):
            if engine == "scalar":
                nc.scalar.activation(rows[t][:, cols], accs[t][:, 0:HALF], ACT.Copy, scale=-0.0625 if t == 0 else 0.0625)
            else:
                nc.vector.tensor_scalar(rows[t][:, cols], accs[t][:, 0:HALF], 0.0625, None, ALU.mult)

        shared = sbuf("shared", [P, Z_CHUNKS[-1] + Z_CHUNKS[0] * PACK // 2], F32)
        c0 = 0
        for c, n in enumerate(Z_CHUNKS):
            last = c == len(Z_CHUNKS) - 1
            if last:
                z = shared[:, 0 : PACK * n].rearrange("p (t j) -> p t j", t=PACK)
            else:
                z = sbuf("z%d" % c, [P, PACK, n], F32)[:]
            for t in range(PACK):
                nc.vector.tensor_tensor(
                    z[:, t, :],
                    ds_half[t][:].indirect(n3_list[:, c0 // 16 : (c0 + n) // 16]),
                    rows[t][:, c0 : c0 + n],
                    ALU.add,
                )
            if c == 0:
                z_bf = shared[:, Z_CHUNKS[-1] :].bitcast(BF16)
            else:
                z_bf = keep.tile([P, n * PACK], BF16, name="z_bf%d" % c, tag="z_bf", align_bytes=64)[:]
            dst = z_bf.rearrange("p (c i t) -> p c t i", i=4, t=PACK)
            src = z.rearrange("p t (c i) -> p c t i", i=4)
            if last:
                nc.vector.tensor_copy(dst, src)
            else:
                nc.scalar.copy(dst, src)
            z_codes = sbuf("z_codes%d" % c, [P, n], U32)
            z_scales = sbuf("z_scales%d" % c, [P, n], U8)
            nc.vector.quantize_mx(out=z_codes[:].bitcast(FP8X4), scales=z_scales[:], in_=z_bf)
            if c0 % HALF == 0:
                accs = [bank() for t in range(PACK)]
            for t in range(PACK):
                product(accs[t][:, c0 % HALF : c0 % HALF + n], t, z_codes[:], z_scales[:])
            c0 += n
            if c0 == HALF:
                nc.scalar.activation(gate[0][:, halves[0]], accs[0][:, 0:HALF], ACT.Sigmoid, scale=0.0625)
                for t in range(PACK):
                    leave_bank(t, accs, halves[0], "scalar")

        out_rows = out.rearrange("(p t) j -> p t j", t=PACK)
        minus_st_copy = [sbuf("minus_st_copy%d" % t, [P, S], F32) for t in range(PACK)]
        result = [sbuf("result%d" % t, [P, S], F32) for t in range(PACK)]

        def gate_of(t):
            nc.scalar.activation(gate[t][:], rows[t][:].indirect(n4_list[:]), ACT.Sigmoid)

        def gated(t):
            nc.vector.scalar_tensor_tensor(st_window[t][:, 0:S], rows[t][:, 0:S], -1.0, gate[t][:], ALU.mult, ALU.mult)

        def difference(t):
            nc.scalar.copy(minus_st_copy[t][:], st_window[t][:, 0:S])
            for cols, entries in zip(halves, list_halves) if t == PACK - 1 else zip(whole, list_whole):
                nc.vector.tensor_tensor(
                    result[t][:, cols], st_window[t][:].indirect(n5_list[:, entries]), minus_st_copy[t][:, cols], ALU.subtract
                )
                nc.sync.dma_start(out_rows[:, t, cols], result[t][:, cols])

        nc.scalar.activation(gate[0][:, halves[1]], accs[0][:, 0:HALF], ACT.Sigmoid, scale=0.0625)
        leave_bank(0, accs, halves[1], "scalar")
        leave_bank(1, accs, halves[1], "vector")
        gate_of(1)
        for cols, entries in zip(halves, list_halves):
            nc.vector.tensor_tensor(st_window[0][:, cols], gate[0][:].indirect(n4_list[:, entries]), rows[0][:, cols], ALU.mult)
        leave_bank(2, accs, halves[1], "vector")
        gated(1)
        difference(0)
        gate_of(2)
        gated(2)
        difference(1)
        leave_bank(3, accs, halves[1], "scalar")
        gate_of(3)
        gated(3)
        difference(2)
        difference(3)
